import numpy as np
import ml_dtypes


def mxq(x, axis, fmt="e4m3"):
    dtype, down = {"e4m3": (ml_dtypes.float8_e4m3fn, 7), "e5m2": (ml_dtypes.float8_e5m2, 14)}[fmt]
    v = np.moveaxis(np.asarray(x, np.float32).astype(ml_dtypes.bfloat16).astype(np.float64), axis, -1)
    blocks = v.reshape(v.shape[:-1] + (-1, 32))
    amax = np.abs(blocks).max(-1, keepdims=True)
    byte = np.maximum(np.where(amax > 0, np.frexp(amax)[1] - 1 + 127, 0) - down, 1)
    scale = np.exp2(byte - 127.0)
    codes = (blocks / scale).astype(np.float32).astype(dtype).astype(np.float64)
    return np.moveaxis((codes * scale).reshape(v.shape), -1, axis)


WIDE = False


def mx_kscale(k):
    if not WIDE:
        return np.ones(k)
    levels = np.array([10, -10, 5, -5, 0])
    if k % 512:
        return np.exp2(np.random.permutation(np.resize(levels, k // 32))).repeat(32)
    a = np.empty((k // 512, 16))
    for p in range(k // 512):
        a[p, :8] = np.random.permutation(np.resize(levels, 8))
        for g in range(8):
            far = levels[np.abs(levels - a[p, g]) >= 10]
            a[p, g + 8] = far[np.random.randint(len(far))]
    return np.exp2(a.ravel()).repeat(32)


BF16 = ml_dtypes.bfloat16


def bf(x):
    return np.asarray(x, np.float32).astype(BF16)


def f64(x):
    return np.asarray(x).astype(np.float64)


E2M1 = np.array([0.0, 0.5, 1.0, 1.5, 2.0, 3.0, 4.0, 6.0, -0.0, -0.5, -1.0, -1.5, -2.0, -3.0, -4.0, -6.0])


def pack_weight(w, fmt):
    k, n = w.shape
    w = f64(bf(w)).reshape(k // 32, 32, n)
    amax = np.abs(w).max(1)
    if fmt == "e4m3":
        byte = np.frexp(amax)[1] - 1 + 127 - 7
    else:
        mant, ex = np.frexp(amax / 6.0)
        byte = np.where(mant > 0.5, ex, ex - 1) + 127
    byte = np.clip(np.where(amax > 0, byte, 1), 1, 254)
    scaled = (w * np.exp2(127.0 - byte)[:, None, :]).reshape(k, n).astype(np.float32)
    by_word = np.ascontiguousarray(scaled.reshape(k // 512, 128, 4, n).transpose(0, 1, 3, 2))
    if fmt == "e4m3":
        words = by_word.astype(ml_dtypes.float8_e4m3fn).view(np.uint8)
    else:
        c = by_word.astype(ml_dtypes.float4_e2m1fn).view(np.uint8) & 0xF
        words = c[..., 0::2] | (c[..., 1::2] << 4)
    return np.ascontiguousarray(words), np.ascontiguousarray(byte.astype(np.uint8).reshape(k // 512, 16, n))


def unpack_weight(words, scales, fmt):
    g, p, n, _ = words.shape
    if fmt == "e4m3":
        vals = np.ascontiguousarray(words).view(ml_dtypes.float8_e4m3fn).astype(np.float64)
    else:
        nib = np.empty((g, p, n, 4), np.uint8)
        nib[..., 0::2] = words & 0xF
        nib[..., 1::2] = words >> 4
        vals = E2M1[nib]
    vals = vals * np.repeat(np.exp2(scales.astype(np.float64) - 127.0), 8, axis=1)[..., None]
    return vals.transpose(0, 1, 3, 2).reshape(g * 512, n)
def pack4(w):
    words, scales = pack_weight(w, "e2m1")
    return words.reshape(words.shape[0], 128, -1), scales


def unpack4(words, scales):
    return unpack_weight(words.reshape(words.shape[0], 128, -1, 2), scales, "e2m1")


E4M3FN = np.array([(-1.0 if i & 128 else 1.0) * ((1.0 + (i & 7) / 8.0) * 2.0 ** (((i >> 3) & 15) - 7) if i & 120 else (i & 7) * 2.0 ** -9) for i in range(256)])


def e4m3fn_bytes(y):
    return np.clip(np.asarray(y, np.float64), -448.0, 448.0).astype(np.float32).astype(ml_dtypes.float8_e4m3fn).view(np.uint8)


def e4m3fn_values(b):
    return E4M3FN[b]


N, D, F, C = 1024, 1024, 1024, 512


def elu(y):
    return np.where(y > 0, y, np.exp(np.minimum(y, 0.0)) - 1.0)


def sigmoid(v):
    return 1.0 / (1.0 + np.exp(-v))


def draw0():
    s, t = mx_kscale(D), mx_kscale(F)
    x = bf(np.random.standard_normal((N, D)) * s)
    w_words, w_scales = pack4(np.random.standard_normal((D, F)) / np.sqrt(D) / s[:, None])
    g = bf((1.0 + 0.1 * np.random.standard_normal(F)) * t)
    v1_words, v1_scales = pack4(np.random.standard_normal((F, C)) / np.sqrt(F) / t[:, None])
    v0_words, v0_scales = pack4(np.random.standard_normal((F, C)) / np.sqrt(F) / t[:, None])
    return {"x": x,
            "w_words": w_words,
            "w_scales": w_scales,
            "g": g,
            "v1_words": v1_words,
            "v1_scales": v1_scales,
            "v0_words": v0_words,
            "v0_scales": v0_scales,
            "a": bf(np.random.standard_normal(F) / np.sqrt(F)),
            "eps": bf(0.3 * np.random.standard_normal(C))}


def core(x, w_words, w_scales, g, v1_words, v1_scales, v0_words, v0_scales, a, eps):
    h = elu(mxq(f64(x), 1, "e4m3") @ unpack4(w_words, w_scales))
    e = sigmoid(np.sum(h * f64(a)[None, :], axis=1))
    z = h * f64(g)[None, :]
    zq = mxq(z, 1, "e4m3")
    q1 = zq @ unpack4(v1_words, v1_scales)
    q0 = zq @ unpack4(v0_words, v0_scales)
    ep = f64(eps)
    t1 = sigmoid(q1 + ep[None, :] / e[:, None])
    t0 = sigmoid(q0 - ep[None, :] / (1.0 - e[:, None]))
    return t1 - t0


def setup_inputs():
    drawn = draw0()
    full = np.asarray(drawn['x']).astype(np.float64)
    scale = (np.abs(full).reshape(1024, 8, 128).max(axis=(2,)) / 448.0).astype(np.float32)
    given = {}
    for key, value in drawn.items():
        if key == 'x':
            given['x_bytes'] = e4m3fn_bytes(full / np.repeat(scale.astype(np.float64), 128, axis=1))
            given['x_scale'] = scale
        else:
            given[key] = value
    return given


def reference(x_bytes, x_scale, w_words, w_scales, g, v1_words, v1_scales, v0_words, v0_scales, a, eps):
    return core(e4m3fn_values(x_bytes) * np.repeat(x_scale.astype(np.float64), 128, axis=1), w_words, w_scales, g, v1_words, v1_scales, v0_words, v0_scales, a, eps)

@@ -1,0 +1,344 @@
+from contextlib import ExitStack
+
+import concourse.mybir as mybir
+from concourse.masks import make_identity
+
+N, D, F, C = 1024, 1024, 1024, 512
+FLOPS = 2 * N * D * F + 2 * 2 * N * F * C
+
+F32 = mybir.dt.float32
+BF16 = mybir.dt.bfloat16
+U32 = mybir.dt.uint32
+I32 = mybir.dt.int32
+U8 = mybir.dt.uint8
+FP8 = mybir.dt.float8_e4m3fn
+FP8X4 = mybir.dt.float8_e4m3fn_x4
+FP4X4 = mybir.dt.float4_e2m1fn_x4
+ALU = mybir.AluOpType
+ACT = mybir.ActivationFunctionType
+
+P = 128
+TILES = N // P
+HALF = 512
+HEAD_V = (4, 4, 5, 6)
+HEAD_B = (0, 0, 1, 0)
+NEXT_V = (7, 0, 3, 1)
+NEXT_B = (0, 0, 0, 0)
+QUOTA = 7
+VFORM = (0, 1, 2, 3, 4, 5)
+LEAD = 3
+PERM_HEAD = 3
+
+
+def tile_dragonnetlogistictargetedeffect_d1p_kernel(
+    tc, x_bytes, x_scale, w_words, w_scales, g, v1_words, v1_scales, v0_words, v0_scales, a, eps, out
+):
+    nc = tc.nc
+    with ExitStack() as ctx:
+        keep = ctx.enter_context(tc.tile_pool(name="keep", bufs=1))
+        work = ctx.enter_context(tc.tile_pool(name="work", bufs=3))
+        banks = ctx.enter_context(tc.psum_pool(name="banks", bufs=7))
+        sbank = ctx.enter_context(tc.psum_pool(name="sbank", bufs=1))
+        ctx.enter_context(tc.manual_schedule())
+
+        warm = keep.tile([P, 1], F32, name="warm")
+        nc.vector.memset(warm[:], 0.0)
+        one = keep.tile([P, 1], F32, name="one")
+        nc.vector.memset(one[:], 1.0)
+        wsr = keep.tile([P, 2 * F], U8, name="wsr", align_bytes=64)
+        nc.vector.memset(wsr[:].bitcast(I32), 0)
+        vs = keep.tile([P, 2 * 2 * C], U8, name="vs", align_bytes=64)
+        nc.vector.memset(vs[:].bitcast(I32), 0)
+
+        x_view = x_bytes.rearrange("(p i) k -> p i k", i=TILES)
+        xs = keep.tile([P, TILES, 8], F32, name="xs")
+        nc.sync.dma_start(out=xs[:], in_=x_scale.rearrange("(p i) j -> p i j", i=TILES))
+        xb = []
+        for pr in range(4):
+            xb.append(keep.tile([P, 2, D], U8, name=f"xb{pr}"))
+        nc.sync.dma_start(out=xb[0][:, 0, :], in_=x_view[:, 0, :])
+        nc.sync.dma_start(out=xb[0][:, 1, :], in_=x_view[:, 1, :])
+        nc.sync.dma_start(out=xb[1][:], in_=x_view[:, 2:4, :])
+
+        wr = keep.tile([P, 2, 2 * F], U8, name="wr", align_bytes=64)
+        w_view = w_words.rearrange("g p b -> p g b")
+        nc.scalar.dma_start(out=wr[:, :, 0:F].bitcast(I32), in_=w_view[:, :, 0:F].bitcast(I32))
+        wsr_rows = wsr[:].bitcast(I32).rearrange("p (g n) -> p g n", g=2)
+        ws_rows = w_scales.bitcast(I32).rearrange("g (q r) n -> r q g n", r=4)
+        for r in range(4):
+            nc.scalar.dma_start(out=wsr_rows[r : 128 : 32], in_=ws_rows[r])
+        nc.scalar.dma_start(out=wr[:, :, F : 2 * F].bitcast(I32), in_=w_view[:, :, F : 2 * F].bitcast(I32))
+        nc.scalar.activation(out=warm[:], in_=warm[:], func=ACT.Exp)
+
+        a_bf = keep.tile([P, 2, 4], BF16, name="a_bf")
+        g_bf = keep.tile([P, 2, 4], BF16, name="g_bf")
+        nc.sync.dma_start(out=a_bf[:], in_=a.rearrange("(h p t) -> p h t", p=P, t=4))
+        nc.sync.dma_start(out=g_bf[:], in_=g.rearrange("(h p t) -> p h t", p=P, t=4))
+        nc.sync.dma_start(out=xb[2][:], in_=x_view[:, 4:6, :])
+        nc.sync.dma_start(out=xb[3][:], in_=x_view[:, 6:8, :])
+        vw = keep.tile([P, 2, 2, 2 * C], U8, name="vw", align_bytes=64)
+        nc.sync.dma_start(out=vw[:, :, 0, :], in_=v1_words.rearrange("g p b -> p g b"))
+        nc.sync.dma_start(out=vw[:, :, 1, :], in_=v0_words.rearrange("g p b -> p g b"))
+        vs_rows = vs[:].bitcast(I32).rearrange("p (v g n) -> p v g n", v=2, g=2)
+        for v, src in ((0, v1_scales), (1, v0_scales)):
+            src_rows = src.bitcast(I32).rearrange("g (q r) n -> r q g n", r=4)
+            for r in range(4):
+                nc.sync.dma_start(out=vs_rows[r : 128 : 32, v], in_=src_rows[r])
+        eps_b = keep.tile([P, C], BF16, name="eps_b")
+        nc.sync.dma_start(out=eps_b[:], in_=eps.partition_broadcast(P))
+
+        ident = keep.tile([P, P], F32, name="ident")
+        make_identity(nc, ident[:])
+        a_f = keep.tile([P, 2, 4], F32, name="a_f")
+        ones = keep.tile([P, P], F32, name="ones")
+        nc.gpsimd.memset(ones[:], 1.0)
+
+        wp = keep.tile([P, 2, 2, 4, 256], U8, name="wp", align_bytes=64)
+        wsp = keep.tile([P, 2, 2, 4, 128], U8, name="wsp", align_bytes=64)
+        xin = [keep.tile([P, 2, HALF * 4], BF16, name=f"xin{h}", align_bytes=64) for h in range(2)]
+        xq = [keep.tile([P, 2, HALF], U32, name=f"xq{h}", align_bytes=64) for h in range(2)]
+        xqs = [keep.tile([P, 2, HALF], U8, name=f"xqs{h}", align_bytes=64) for h in range(2)]
+        zq = [keep.tile([P, 2, HALF], U32, name=f"zq{h}", align_bytes=64) for h in range(2)]
+        zqs = [keep.tile([P, 2, HALF], U8, name=f"zqs{h}", align_bytes=64) for h in range(2)]
+        s_ps = sbank.tile([P, TILES + 1, 8], F32, name="s_ps")
+
+        xw = {}
+        bank_of = {}
+        e_of = {}
+        em_of = {}
+        h_of = {}
+        zin_of = {}
+        t_of = {}
+
+        def widen(i, j, on_vector):
+            if i not in xw:
+                xw[i] = work.tile([P, D], BF16, name="xw", bufs=4, align_bytes=64)
+            src = xb[i // 2][:, i % 2, j * P : (j + 1) * P].bitcast(FP8)
+            dst = xw[i][:, j * P : (j + 1) * P]
+            if on_vector:
+                nc.vector.tensor_scalar(out=dst, in0=src, scalar1=xs[:, i, j : j + 1], scalar2=None, op0=ALU.mult)
+            else:
+                nc.scalar.activation(out=dst, in_=src, func=ACT.Copy, scale=xs[:, i, j : j + 1])
+
+        def turn(i):
+            bank = banks.tile([P, 512], F32, name="bank")
+            t_of[i] = bank
+            words = xw[i][:].bitcast(F32)
+            for gg in range(2):
+                for u in range(2):
+                    c = (2 * gg + u) * P
+                    nc.tensor.transpose(bank[:, c : c + P], words[:, 256 * gg + u : 256 * (gg + 1) : 2], ident[:])
+
+        def untangle(i, on_vector):
+            half, il = divmod(i, 4)
+            dst = xin[half][:].bitcast(F32).rearrange("p g (n u) -> p g n u", u=2)[:, :, il * P : (il + 1) * P, :]
+            src = t_of[i][:].rearrange("p (g u n) -> p g n u", g=2, u=2)
+            if on_vector:
+                nc.vector.tensor_copy(out=dst, in_=src)
+            else:
+                nc.scalar.copy(out=dst, in_=src)
+
+        def quant_x(pair):
+            half, pl = divmod(pair, 2)
+            for gg in range(2):
+                nc.vector.quantize_mx(
+                    out=xq[half][:, gg, pl * 256 : (pl + 1) * 256].bitcast(FP8X4),
+                    scales=xqs[half][:, gg, pl * 256 : (pl + 1) * 256],
+                    in_=xin[half][:, gg, pl * 1024 : (pl + 1) * 1024],
+                )
+
+        def permute_w(k, engine):
+            G, t = divmod(k, 4)
+            src = wr[:, :, G * F : (G + 1) * F].rearrange("p g (m t b) -> p g t m b", t=4, b=2)[:, :, t]
+            engine.tensor_copy(out=wp[:, :, G, t, :].rearrange("p g (m b) -> p g m b", b=2), in_=src)
+            src = wsr[:].rearrange("p (g h m t) -> p g h t m", g=2, h=2, t=4)[:, :, G, t]
+            engine.tensor_copy(out=wsp[:, :, G, t, :], in_=src)
+
+        def mx1(u):
+            half, k = divmod(u, 8)
+            G, t = divmod(k, 4)
+            bank = banks.tile([P, 512], F32, name="bank")
+            bank_of[u] = bank
+            for gg in range(2):
+                nc.tensor.matmul_mx(
+                    out=bank[:],
+                    lhsT=wp[:, gg, G, t, :].bitcast(FP4X4),
+                    lhsT_scale=wsp[:, gg, G, t, :],
+                    rhs=xq[half][:, gg, :].bitcast(FP8X4),
+                    rhs_scale=xqs[half][:, gg, :],
+                    start=gg == 0,
+                    stop=gg == 1,
+                )
+
+        def exp(u):
+            e = work.tile([P, HALF], F32, name="e")
+            e_of[u] = e
+            nc.scalar.activation(out=e[:], in_=bank_of[u][:], func=ACT.Exp)
+
+        def plus1(u):
+            em = work.tile([P, HALF], F32, name="em")
+            em_of[u] = em
+            nc.scalar.activation(out=em[:], in_=bank_of[u][:], func=ACT.Identity, bias=one[:])
+
+        def clamp(u):
+            em = work.tile([P, HALF], F32, name="em")
+            em_of[u] = em
+            nc.vector.tensor_scalar(out=em[:], in0=e_of[u][:], scalar1=1.0, scalar2=None, op0=ALU.min)
+
+        def elu1(u):
+            if u % 4 == 0:
+                h_of[u // 4] = work.tile([P, 4, HALF], F32, name="h")
+            dst = h_of[u // 4][:, u % 4, :]
+            if u in VFORM:
+                nc.vector.scalar_tensor_tensor(
+                    out=dst, in0=bank_of[u][:], scalar=0.0, in1=em_of[u][:], op0=ALU.max, op1=ALU.add
+                )
+            else:
+                nc.vector.scalar_tensor_tensor(
+                    out=dst, in0=e_of[u][:], scalar=1.0, in1=em_of[u][:], op0=ALU.min, op1=ALU.max
+                )
+
+        def asum(u):
+            half, k = divmod(u, 8)
+            G, t = divmod(k, 4)
+            for il in range(4):
+                nc.tensor.matmul(
+                    s_ps[:, half * 4 + il, k : k + 1],
+                    lhsT=h_of[u // 4][:, t, il * P : (il + 1) * P],
+                    rhs=a_f[:, G, t : t + 1],
+                    start=True,
+                    stop=True,
+                )
+
+        def gain(grp, il):
+            G = grp % 2
+            zin = work.tile([P, P, 4], BF16, name="zin", bufs=4, align_bytes=64)
+            zin_of[grp, il] = zin
+            nc.vector.scalar_tensor_tensor(
+                out=zin[:],
+                in0=h_of[grp][:].rearrange("p t n -> p n t")[:, il * P : (il + 1) * P, :],
+                scalar=-1.0,
+                in1=g_bf[:, G : G + 1, :].to_broadcast([P, P, 4]),
+                op0=ALU.add,
+                op1=ALU.mult,
+            )
+
+        def quant_z(grp, il):
+            half, G = divmod(grp, 2)
+            cols = slice(il * P, (il + 1) * P)
+            nc.vector.quantize_mx(
+                out=zq[half][:, G, cols].bitcast(FP8X4),
+                scales=zqs[half][:, G, cols],
+                in_=zin_of[grp, il][:].rearrange("p n t -> p (n t)"),
+            )
+
+        for i in range(4):
+            for j in range(8):
+                widen(i, j, j < HEAD_V[i])
+            turn(i)
+        for k in range(PERM_HEAD):
+            permute_w(k, nc.vector)
+        for i in range(4):
+            untangle(i, HEAD_B[i] == 1)
+        quant_x(0)
+        quant_x(1)
+        nc.vector.tensor_copy(out=a_f[:], in_=a_bf[:])
+        for u in range(LEAD):
+            mx1(u)
+        nc.tensor.matmul(s_ps[:, TILES, :], lhsT=ones[:], rhs=a_f[:].rearrange("p h t -> p (h t)"), start=True, stop=True)
+
+        s_sum = keep.tile([P, TILES + 1], F32, name="s_sum")
+        s_dev = keep.tile([P, TILES], F32, name="s_dev")
+        ee = keep.tile([P, 2, TILES], F32, name="ee")
+        rec = keep.tile([P, 2, TILES], F32, name="rec")
+        rr = keep.tile([P, 2, TILES], F32, name="rr")
+        blocks = [(i, j) for i in range(4, 8) for j in range(8)]
+        turned = []
+        units = 16
+        for u in range(units + 6):
+            if u < units:
+                exp(u)
+                if u not in VFORM:
+                    plus1(u)
+            ready = list(turned)
+            turned.clear()
+            for i in ready:
+                untangle(i, NEXT_B[i - 4] == 1)
+            quota = QUOTA
+            while blocks and quota > 0:
+                i, j = blocks.pop(0)
+                widen(i, j, j < NEXT_V[i - 4])
+                quota -= 1
+                if j == 7:
+                    turn(i)
+                    turned.append(i)
+            if 1 <= u <= units:
+                elu1(u - 1)
+            piece = u - 5
+            if 1 <= piece < 17:
+                quant_z((piece - 1) // 4, (piece - 1) % 4)
+            if 0 <= piece < 16:
+                gain(piece // 4, piece % 4)
+            if u in VFORM:
+                clamp(u)
+            for i in ready:
+                if i % 2 == 1:
+                    quant_x(i // 2)
+            if PERM_HEAD <= u + PERM_HEAD < 8:
+                permute_w(u + PERM_HEAD, nc.gpsimd)
+            if u + LEAD < units:
+                mx1(u + LEAD)
+            if 1 <= u <= units:
+                asum(u - 1)
+            if u == units + 1:
+                nc.vector.tensor_reduce(out=s_sum[:], in_=s_ps[:], axis=mybir.AxisListType.X, op=ALU.add)
+            if u == units + 2:
+                nc.vector.tensor_scalar(
+                    out=s_dev[:], in0=s_sum[:, 0:TILES], scalar1=s_sum[:, TILES : TILES + 1], scalar2=None,
+                    op0=ALU.subtract,
+                )
+                nc.scalar.activation(out=ee[:, 0, :], in_=s_dev[:], func=ACT.Sigmoid)
+                nc.scalar.activation(out=ee[:, 1, :], in_=s_dev[:], func=ACT.Sigmoid, scale=-1.0)
+            if u == units + 3:
+                nc.vector.reciprocal(out=rec[:], in_=ee[:])
+            if u == units + 4:
+                for v, sign in ((0, 1.0), (1, -1.0)):
+                    nc.vector.tensor_scalar(
+                        out=rr[:, v, :], in0=rec[:, v, :], scalar1=3.0e38, scalar2=sign, op0=ALU.min, op1=ALU.mult
+                    )
+
+        out_view = out.rearrange("(p i) c -> p i c", i=TILES)
+        q_of = {}
+        arg_of = {}
+        for i in range(TILES):
+            if True:
+                half, il = divmod(i, 4)
+                cols = slice(il * P, (il + 1) * P)
+                for v in range(2):
+                    bank = banks.tile([P, 512], F32, name="bank")
+                    q_of[i, v] = bank
+                    for G in range(2):
+                        nc.tensor.matmul_mx(
+                            out=bank[:],
+                            lhsT=zq[half][:, G, cols].bitcast(FP8X4),
+                            lhsT_scale=zqs[half][:, G, cols],
+                            rhs=vw[:, G, v, :].bitcast(FP4X4),
+                            rhs_scale=vs[:].rearrange("p (v g n) -> p v g n", v=2, g=2)[:, v, G, :],
+                            start=G == 0,
+                            stop=G == 1,
+                        )
+                arg = work.tile([P, 2, C], F32, name="arg")
+                arg_of[i] = arg
+                for v in range(2):
+                    nc.vector.scalar_tensor_tensor(
+                        out=arg[:, v, :], in0=eps_b[:], scalar=rr[:, v, i : i + 1], in1=q_of[i, v][:],
+                        op0=ALU.mult, op1=ALU.add,
+                    )
+                tt = work.tile([P, 2, C], F32, name="tt")
+                nc.scalar.activation(out=tt[:], in_=arg[:], func=ACT.Sigmoid)
+                o = work.tile([P, C], F32, name="o")
+                if i == TILES - 1:
+                    nc.vector.tensor_sub(out=o[:], in0=tt[:, 0, :], in1=tt[:, 1, :])
+                else:
+                    nc.gpsimd.tensor_sub(out=o[:], in0=tt[:, 0, :], in1=tt[:, 1, :])
+                nc.sync.dma_start(out=out_view[:, i, :], in_=o[:])

@@ -20,14 +20,17 @@ ACT = mybir.ActivationFunctionType
 P = 128
 TILES = N // P
 HALF = 512
-HEAD_V = (4, 4, 5, 6)
-HEAD_B = (0, 0, 1, 0)
-NEXT_V = (7, 0, 3, 1)
-NEXT_B = (0, 0, 0, 0)
-QUOTA = 7
-VFORM = (0, 1, 2, 3, 4, 5)
-LEAD = 3
-PERM_HEAD = 3
+UNITS = 16
+SPLIT = TILES // 2
+
+A_V = (5, 4, 5, 4, 0, 2, 8, 5)
+B_V = (0, 0, 0, 0, 0, 0, 1, 0)
+LEAD = 2
+QUOTA = 8
+EARLY = 3
+PERM_MID = 6
+PERM_AT = 8
+AHEAD = 20
 
 
 def tile_dragonnetlogistictargetedeffect_d1p_kernel(
@@ -37,7 +40,7 @@ def tile_dragonnetlogistictargetedeffect_d1p_kernel(
     with ExitStack() as ctx:
         keep = ctx.enter_context(tc.tile_pool(name="keep", bufs=1))
         work = ctx.enter_context(tc.tile_pool(name="work", bufs=3))
-        banks = ctx.enter_context(tc.psum_pool(name="banks", bufs=7))
+        banks = ctx.enter_context(tc.psum_pool(name="banks", bufs=6))
         sbank = ctx.enter_context(tc.psum_pool(name="sbank", bufs=1))
         ctx.enter_context(tc.manual_schedule())
 
@@ -100,15 +103,16 @@ def tile_dragonnetlogistictargetedeffect_d1p_kernel(
         xqs = [keep.tile([P, 2, HALF], U8, name=f"xqs{h}", align_bytes=64) for h in range(2)]
         zq = [keep.tile([P, 2, HALF], U32, name=f"zq{h}", align_bytes=64) for h in range(2)]
         zqs = [keep.tile([P, 2, HALF], U8, name=f"zqs{h}", align_bytes=64) for h in range(2)]
-        s_ps = sbank.tile([P, TILES + 1, 8], F32, name="s_ps")
+        s_early = sbank.tile([P, SPLIT + 1, 8], F32, name="s_early")
+        s_late = sbank.tile([P, TILES - SPLIT, 8], F32, name="s_late")
 
         xw = {}
+        t_of = {}
         bank_of = {}
         e_of = {}
-        em_of = {}
+        y1_of = {}
         h_of = {}
         zin_of = {}
-        t_of = {}
 
         def widen(i, j, on_vector):
             if i not in xw:
@@ -171,174 +175,229 @@ def tile_dragonnetlogistictargetedeffect_d1p_kernel(
                 )
 
         def exp(u):
-            e = work.tile([P, HALF], F32, name="e")
-            e_of[u] = e
-            nc.scalar.activation(out=e[:], in_=bank_of[u][:], func=ACT.Exp)
+            pair, k = divmod(u, 2)
+            if k == 0:
+                e_of[pair] = work.tile([P, 2, HALF], F32, name="e")
+                y1_of[pair] = work.tile([P, 2, HALF], F32, name="y1")
+            nc.scalar.activation(out=e_of[pair][:, k, :], in_=bank_of[u][:], func=ACT.Exp)
+            nc.scalar.activation(out=y1_of[pair][:, k, :], in_=bank_of[u][:], func=ACT.Identity, bias=one[:])
 
-        def plus1(u):
-            em = work.tile([P, HALF], F32, name="em")
-            em_of[u] = em
-            nc.scalar.activation(out=em[:], in_=bank_of[u][:], func=ACT.Identity, bias=one[:])
-
-        def clamp(u):
-            em = work.tile([P, HALF], F32, name="em")
-            em_of[u] = em
-            nc.vector.tensor_scalar(out=em[:], in0=e_of[u][:], scalar1=1.0, scalar2=None, op0=ALU.min)
-
-        def elu1(u):
-            if u % 4 == 0:
-                h_of[u // 4] = work.tile([P, 4, HALF], F32, name="h")
-            dst = h_of[u // 4][:, u % 4, :]
-            if u in VFORM:
-                nc.vector.scalar_tensor_tensor(
-                    out=dst, in0=bank_of[u][:], scalar=0.0, in1=em_of[u][:], op0=ALU.max, op1=ALU.add
-                )
-            else:
-                nc.vector.scalar_tensor_tensor(
-                    out=dst, in0=e_of[u][:], scalar=1.0, in1=em_of[u][:], op0=ALU.min, op1=ALU.max
-                )
+        def elu1(pair, part):
+            grp, k = divmod(pair, 2)
+            if k == 0 and part.start == 0:
+                h_of[grp] = work.tile([P, 4, HALF], F32, name="h")
+            nc.vector.scalar_tensor_tensor(
+                out=h_of[grp][:, 2 * k + part.start : 2 * k + part.stop, :],
+                in0=e_of[pair][:, part, :],
+                scalar=1.0,
+                in1=y1_of[pair][:, part, :],
+                op0=ALU.min,
+                op1=ALU.max,
+            )
 
         def asum(u):
-            half, k = divmod(u, 8)
-            G, t = divmod(k, 4)
+            grp, t = divmod(u, 4)
+            half, G = divmod(grp, 2)
+            sums = (s_early, s_late)[half]
             for il in range(4):
                 nc.tensor.matmul(
-                    s_ps[:, half * 4 + il, k : k + 1],
-                    lhsT=h_of[u // 4][:, t, il * P : (il + 1) * P],
+                    sums[:, il, 4 * G + t : 4 * G + t + 1],
+                    lhsT=h_of[grp][:, t, il * P : (il + 1) * P],
                     rhs=a_f[:, G, t : t + 1],
                     start=True,
                     stop=True,
                 )
 
-        def gain(grp, il):
+        def gain(grp, lo, hi):
             G = grp % 2
-            zin = work.tile([P, P, 4], BF16, name="zin", bufs=4, align_bytes=64)
-            zin_of[grp, il] = zin
+            if lo == 0:
+                zin_of[grp] = work.tile([P, HALF, 4], BF16, name="zin", align_bytes=64)
             nc.vector.scalar_tensor_tensor(
-                out=zin[:],
-                in0=h_of[grp][:].rearrange("p t n -> p n t")[:, il * P : (il + 1) * P, :],
+                out=zin_of[grp][:, lo:hi, :],
+                in0=h_of[grp][:].rearrange("p t n -> p n t")[:, lo:hi, :],
                 scalar=-1.0,
-                in1=g_bf[:, G : G + 1, :].to_broadcast([P, P, 4]),
+                in1=g_bf[:, G : G + 1, :].to_broadcast([P, hi - lo, 4]),
                 op0=ALU.add,
                 op1=ALU.mult,
             )
 
-        def quant_z(grp, il):
+        def quant_z(grp, lo, hi):
             half, G = divmod(grp, 2)
-            cols = slice(il * P, (il + 1) * P)
             nc.vector.quantize_mx(
-                out=zq[half][:, G, cols].bitcast(FP8X4),
-                scales=zqs[half][:, G, cols],
-                in_=zin_of[grp, il][:].rearrange("p n t -> p (n t)"),
+                out=zq[half][:, G, lo:hi].bitcast(FP8X4),
+                scales=zqs[half][:, G, lo:hi],
+                in_=zin_of[grp][:, lo:hi, :].rearrange("p n t -> p (n t)"),
             )
 
-        for i in range(4):
-            for j in range(8):
-                widen(i, j, j < HEAD_V[i])
-            turn(i)
-        for k in range(PERM_HEAD):
-            permute_w(k, nc.vector)
-        for i in range(4):
-            untangle(i, HEAD_B[i] == 1)
-        quant_x(0)
-        quant_x(1)
-        nc.vector.tensor_copy(out=a_f[:], in_=a_bf[:])
-        for u in range(LEAD):
-            mx1(u)
-        nc.tensor.matmul(s_ps[:, TILES, :], lhsT=ones[:], rhs=a_f[:].rearrange("p h t -> p (h t)"), start=True, stop=True)
-
-        s_sum = keep.tile([P, TILES + 1], F32, name="s_sum")
-        s_dev = keep.tile([P, TILES], F32, name="s_dev")
-        ee = keep.tile([P, 2, TILES], F32, name="ee")
-        rec = keep.tile([P, 2, TILES], F32, name="rec")
-        rr = keep.tile([P, 2, TILES], F32, name="rr")
-        blocks = [(i, j) for i in range(4, 8) for j in range(8)]
+        blocks = [(i, j) for i in range(TILES) for j in range(8)]
         turned = []
-        units = 16
-        for u in range(units + 6):
-            if u < units:
-                exp(u)
-                if u not in VFORM:
-                    plus1(u)
-            ready = list(turned)
-            turned.clear()
-            for i in ready:
-                untangle(i, NEXT_B[i - 4] == 1)
-            quota = QUOTA
+        copied = []
+
+        def widen_next(quota):
             while blocks and quota > 0:
                 i, j = blocks.pop(0)
-                widen(i, j, j < NEXT_V[i - 4])
+                widen(i, j, j < A_V[i])
                 quota -= 1
                 if j == 7:
                     turn(i)
                     turned.append(i)
-            if 1 <= u <= units:
-                elu1(u - 1)
-            piece = u - 5
-            if 1 <= piece < 17:
-                quant_z((piece - 1) // 4, (piece - 1) % 4)
-            if 0 <= piece < 16:
-                gain(piece // 4, piece % 4)
-            if u in VFORM:
-                clamp(u)
-            for i in ready:
-                if i % 2 == 1:
-                    quant_x(i // 2)
-            if PERM_HEAD <= u + PERM_HEAD < 8:
-                permute_w(u + PERM_HEAD, nc.gpsimd)
-            if u + LEAD < units:
-                mx1(u + LEAD)
-            if 1 <= u <= units:
-                asum(u - 1)
-            if u == units + 1:
-                nc.vector.tensor_reduce(out=s_sum[:], in_=s_ps[:], axis=mybir.AxisListType.X, op=ALU.add)
-            if u == units + 2:
+
+        for k in range(PERM_AT, 8):
+            permute_w(k, nc.gpsimd)
+        widen_next(32)
+        for k in range(EARLY):
+            permute_w(k, nc.vector)
+        for i in range(4):
+            untangle(i, B_V[i] == 1)
+            if i == 2:
+                quant_x(0)
+        turned.clear()
+        quant_x(1)
+        for k in range(EARLY, PERM_MID):
+            permute_w(k, nc.vector)
+        nc.vector.tensor_copy(out=a_f[:], in_=a_bf[:])
+        for u in range(LEAD):
+            mx1(u)
+        for k in range(PERM_MID, PERM_AT):
+            permute_w(k, nc.vector)
+        widen_next(AHEAD)
+
+        rr = keep.tile([P, 2, 2, 4], F32, name="rr")
+        nr = keep.tile([P, 2, 4], F32, name="nr")
+        sum_of = {}
+        lim_of = {}
+        prob_of = {}
+
+        def sum_up(late):
+            n = TILES - SPLIT if late else SPLIT + 1
+            sums = s_late if late else s_early
+            sum_of[late] = keep.tile([P, n], F32, name="sum_late" if late else "sum_early")
+            nc.vector.tensor_reduce(out=sum_of[late][:], in_=sums[:], axis=mybir.AxisListType.X, op=ALU.add)
+
+        def limit(late):
+            total = sum_of[False][:, SPLIT : SPLIT + 1]
+            lim = keep.tile([P, 2, 4], F32, name="lim_late" if late else "lim_early")
+            lim_of[late] = lim
+            for v, (bound, op) in enumerate(((-86.0, ALU.max), (86.0, ALU.min))):
                 nc.vector.tensor_scalar(
-                    out=s_dev[:], in0=s_sum[:, 0:TILES], scalar1=s_sum[:, TILES : TILES + 1], scalar2=None,
-                    op0=ALU.subtract,
+                    out=lim[:, v, :], in0=sum_of[late][:, 0:4], scalar1=total, scalar2=bound, op0=ALU.subtract, op1=op
                 )
-                nc.scalar.activation(out=ee[:, 0, :], in_=s_dev[:], func=ACT.Sigmoid)
-                nc.scalar.activation(out=ee[:, 1, :], in_=s_dev[:], func=ACT.Sigmoid, scale=-1.0)
-            if u == units + 3:
-                nc.vector.reciprocal(out=rec[:], in_=ee[:])
-            if u == units + 4:
-                for v, sign in ((0, 1.0), (1, -1.0)):
-                    nc.vector.tensor_scalar(
-                        out=rr[:, v, :], in0=rec[:, v, :], scalar1=3.0e38, scalar2=sign, op0=ALU.min, op1=ALU.mult
-                    )
+
+        def probabilities(late):
+            prob = keep.tile([P, 2, 4], F32, name="prob_late" if late else "prob_early")
+            prob_of[late] = prob
+            for v, sign in enumerate((1.0, -1.0)):
+                nc.scalar.activation(out=prob[:, v, :], in_=lim_of[late][:, v, :], func=ACT.Sigmoid, scale=sign)
+
+        def factors(late):
+            rec = rr[:, late, :, :]
+            nc.vector.reciprocal(out=rec, in_=prob_of[late][:])
+            nc.vector.tensor_scalar(out=nr[:, late, :], in0=rr[:, late, 1, :], scalar1=-1.0, scalar2=None, op0=ALU.mult)
 
         out_view = out.rearrange("(p i) c -> p i c", i=TILES)
+        vs_view = vs[:].rearrange("p (v g n) -> p v g n", v=2, g=2)
         q_of = {}
         arg_of = {}
-        for i in range(TILES):
-            if True:
-                half, il = divmod(i, 4)
-                cols = slice(il * P, (il + 1) * P)
-                for v in range(2):
-                    bank = banks.tile([P, 512], F32, name="bank")
-                    q_of[i, v] = bank
-                    for G in range(2):
-                        nc.tensor.matmul_mx(
-                            out=bank[:],
-                            lhsT=zq[half][:, G, cols].bitcast(FP8X4),
-                            lhsT_scale=zqs[half][:, G, cols],
-                            rhs=vw[:, G, v, :].bitcast(FP4X4),
-                            rhs_scale=vs[:].rearrange("p (v g n) -> p v g n", v=2, g=2)[:, v, G, :],
-                            start=G == 0,
-                            stop=G == 1,
-                        )
-                arg = work.tile([P, 2, C], F32, name="arg")
-                arg_of[i] = arg
-                for v in range(2):
-                    nc.vector.scalar_tensor_tensor(
-                        out=arg[:, v, :], in0=eps_b[:], scalar=rr[:, v, i : i + 1], in1=q_of[i, v][:],
-                        op0=ALU.mult, op1=ALU.add,
+
+        def mx2(i):
+            for v in range(2):
+                bank = banks.tile([P, 512], F32, name="bank")
+                q_of[i, v] = bank
+                for G in range(2):
+                    nc.tensor.matmul_mx(
+                        out=bank[:],
+                        lhsT=zq[i // 4][:, G, i % 4 * P : (i % 4 + 1) * P].bitcast(FP8X4),
+                        lhsT_scale=zqs[i // 4][:, G, i % 4 * P : (i % 4 + 1) * P],
+                        rhs=vw[:, G, v, :].bitcast(FP4X4),
+                        rhs_scale=vs_view[:, v, G, :],
+                        start=G == 0,
+                        stop=G == 1,
                     )
-                tt = work.tile([P, 2, C], F32, name="tt")
-                nc.scalar.activation(out=tt[:], in_=arg[:], func=ACT.Sigmoid)
-                o = work.tile([P, C], F32, name="o")
-                if i == TILES - 1:
-                    nc.vector.tensor_sub(out=o[:], in0=tt[:, 0, :], in1=tt[:, 1, :])
-                else:
-                    nc.gpsimd.tensor_sub(out=o[:], in0=tt[:, 0, :], in1=tt[:, 1, :])
-                nc.sync.dma_start(out=out_view[:, i, :], in_=o[:])
+
+        def arguments(i, cols):
+            late, il = divmod(i, 4)
+            arg = work.tile([P, 2, cols.stop - cols.start], F32, name="arg", bufs=4)
+            arg_of[i, cols.start] = arg
+            for v, factor in enumerate((rr[:, late, 0, il : il + 1], nr[:, late, il : il + 1])):
+                nc.vector.scalar_tensor_tensor(
+                    out=arg[:, v, :], in0=eps_b[:, cols], scalar=factor, in1=q_of[i, v][:, cols],
+                    op0=ALU.mult, op1=ALU.add,
+                )
+
+        def effect(i, cols, engine):
+            width = cols.stop - cols.start
+            tt = work.tile([P, 2, width], F32, name="tt", bufs=4)
+            nc.scalar.activation(out=tt[:], in_=arg_of[i, cols.start][:], func=ACT.Sigmoid)
+            o = work.tile([P, width], F32, name="o", bufs=9)
+            engine.tensor_sub(out=o[:], in0=tt[:, 0, :], in1=tt[:, 1, :])
+            nc.sync.dma_start(out=out_view[:, i, cols], in_=o[:])
+
+        for u in range(UNITS + 6):
+            if u < UNITS:
+                exp(u)
+            for i in turned:
+                untangle(i, B_V[i] == 1)
+                copied.append(i)
+            turned.clear()
+            widen_next(QUOTA)
+            last = u > UNITS
+            if u % 2 == 0 and 2 <= u < UNITS:
+                elu1(u // 2 - 1, slice(0, 2))
+            if u in (UNITS - 1, UNITS):
+                elu1(UNITS // 2 - 1, slice(u - UNITS + 1, u - UNITS + 2))
+            piece, odd = divmod(u - 5, 2)
+            if odd == 1 and 0 <= piece < 6:
+                quant_z(piece // 2, (piece % 2) * 256, (piece % 2 + 1) * 256)
+            if UNITS + 2 <= u < UNITS + 6:
+                quant_z(3, (u - UNITS - 2) * P, (u - UNITS - 1) * P)
+            for i in copied:
+                if i % 2 == 1:
+                    quant_x(i // 2)
+            copied.clear()
+            if odd == 0 and 0 <= piece < 6:
+                gain(piece // 2, (piece % 2) * 256, (piece % 2 + 1) * 256)
+            if UNITS + 1 <= u < UNITS + 5:
+                gain(3, (u - UNITS - 1) * P, (u - UNITS) * P)
+            if u + LEAD < UNITS:
+                mx1(u + LEAD)
+            if u % 2 == 0 and 2 <= u < UNITS:
+                asum(u - 2)
+                asum(u - 1)
+            if u in (UNITS - 1, UNITS):
+                asum(u - 1)
+            if u == 3:
+                nc.tensor.matmul(
+                    s_early[:, SPLIT, :], lhsT=ones[:], rhs=a_f[:].rearrange("p h t -> p (h t)"), start=True, stop=True
+                )
+            if u == 10:
+                sum_up(False)
+            if u == 11:
+                limit(False)
+            if u == UNITS - 1:
+                probabilities(False)
+            if u == UNITS + 1:
+                factors(False)
+                mx2(0)
+            if u == UNITS + 2:
+                sum_up(True)
+                arguments(0, slice(0, C))
+                effect(0, slice(0, C), nc.gpsimd)
+                mx2(1)
+            if u == UNITS + 3:
+                limit(True)
+                probabilities(True)
+            if u == UNITS + 4:
+                arguments(1, slice(0, C))
+                effect(1, slice(0, C), nc.gpsimd)
+                mx2(2)
+        factors(True)
+
+        for i in range(2, TILES - 1):
+            mx2(i + 1)
+            arguments(i, slice(0, C))
+            effect(i, slice(0, C), nc.gpsimd)
+        parts = [slice(0, C // 2), slice(C // 2, C)]
+        for cols in parts:
+            arguments(TILES - 1, cols)
+        for cols in parts:
+            effect(TILES - 1, cols, nc.vector)

@@ -25,7 +25,11 @@ SPLIT = TILES // 2
 
 A_V = (5, 4, 5, 4, 0, 2, 8, 5)
 B_V = (0, 0, 0, 0, 0, 0, 1, 0)
-LEAD = 2
+LEAD = 3
+WIDE = 64
+RATE = 3
+RATE_END = 5
+SUM_AT = 13
 QUOTA = 8
 EARLY = 3
 PERM_MID = 6
@@ -103,8 +107,8 @@ def tile_dragonnetlogistictargetedeffect_d1p_kernel(
         xqs = [keep.tile([P, 2, HALF], U8, name=f"xqs{h}", align_bytes=64) for h in range(2)]
         zq = [keep.tile([P, 2, HALF], U32, name=f"zq{h}", align_bytes=64) for h in range(2)]
         zqs = [keep.tile([P, 2, HALF], U8, name=f"zqs{h}", align_bytes=64) for h in range(2)]
-        s_early = sbank.tile([P, SPLIT + 1, 8], F32, name="s_early")
-        s_late = sbank.tile([P, TILES - SPLIT, 8], F32, name="s_late")
+        s_early = sbank.tile([P, 512], F32, name="s_early")
+        s_late = sbank.tile([P, 512], F32, name="s_late")
 
         xw = {}
         t_of = {}
@@ -185,7 +189,7 @@ def tile_dragonnetlogistictargetedeffect_d1p_kernel(
         def elu1(pair, part):
             grp, k = divmod(pair, 2)
             if k == 0 and part.start == 0:
-                h_of[grp] = work.tile([P, 4, HALF], F32, name="h")
+                h_of[grp] = work.tile([P, 4, HALF], F32, name="h", bufs=4)
             nc.vector.scalar_tensor_tensor(
                 out=h_of[grp][:, 2 * k + part.start : 2 * k + part.stop, :],
                 in0=e_of[pair][:, part, :],
@@ -195,15 +199,16 @@ def tile_dragonnetlogistictargetedeffect_d1p_kernel(
                 op1=ALU.max,
             )
 
-        def asum(u):
+        def asum(u, il):
             grp, t = divmod(u, 4)
             half, G = divmod(grp, 2)
             sums = (s_early, s_late)[half]
-            for il in range(4):
+            if True:
+                col = (4 * G + t) * 4 + il
                 nc.tensor.matmul(
-                    sums[:, il, 4 * G + t : 4 * G + t + 1],
+                    sums[:, col : col + WIDE],
                     lhsT=h_of[grp][:, t, il * P : (il + 1) * P],
-                    rhs=a_f[:, G, t : t + 1],
+                    rhs=a_f[:, G, t : t + 1].to_broadcast([P, WIDE]),
                     start=True,
                     stop=True,
                 )
@@ -269,13 +274,22 @@ def tile_dragonnetlogistictargetedeffect_d1p_kernel(
         prob_of = {}
 
         def sum_up(late):
-            n = TILES - SPLIT if late else SPLIT + 1
+            assert not [w for w in waiting if w[0] // 8 == late]
             sums = s_late if late else s_early
-            sum_of[late] = keep.tile([P, n], F32, name="sum_late" if late else "sum_early")
-            nc.vector.tensor_reduce(out=sum_of[late][:], in_=sums[:], axis=mybir.AxisListType.X, op=ALU.add)
+            sum_of[late] = keep.tile([P, 5], F32, name="sum_late" if late else "sum_early")
+            nc.vector.tensor_reduce(
+                out=sum_of[late][:, 0:4],
+                in_=sums[:, 0:32].rearrange("p (k i) -> p i k", i=4),
+                axis=mybir.AxisListType.X,
+                op=ALU.add,
+            )
+            if not late:
+                nc.vector.tensor_reduce(
+                    out=sum_of[late][:, 4:5], in_=sums[:, 256:264], axis=mybir.AxisListType.X, op=ALU.add
+                )
 
         def limit(late):
-            total = sum_of[False][:, SPLIT : SPLIT + 1]
+            total = sum_of[False][:, 4:5]
             lim = keep.tile([P, 2, 4], F32, name="lim_late" if late else "lim_early")
             lim_of[late] = lim
             for v, (bound, op) in enumerate(((-86.0, ALU.max), (86.0, ALU.min))):
@@ -332,6 +346,14 @@ def tile_dragonnetlogistictargetedeffect_d1p_kernel(
             engine.tensor_sub(out=o[:], in0=tt[:, 0, :], in1=tt[:, 1, :])
             nc.sync.dma_start(out=out_view[:, i, cols], in_=o[:])
 
+        waiting = []
+
+        def asum_next(quota):
+            while waiting and quota > 0:
+                u, il = waiting.pop(0)
+                asum(u, il)
+                quota -= 1
+
         for u in range(UNITS + 6):
             if u < UNITS:
                 exp(u)
@@ -361,17 +383,17 @@ def tile_dragonnetlogistictargetedeffect_d1p_kernel(
             if u + LEAD < UNITS:
                 mx1(u + LEAD)
             if u % 2 == 0 and 2 <= u < UNITS:
-                asum(u - 2)
-                asum(u - 1)
+                waiting.extend((v, il) for v in (u - 2, u - 1) for il in range(4))
             if u in (UNITS - 1, UNITS):
-                asum(u - 1)
+                waiting.extend((u - 1, il) for il in range(4))
+            asum_next(RATE if u < UNITS else RATE_END)
             if u == 3:
                 nc.tensor.matmul(
-                    s_early[:, SPLIT, :], lhsT=ones[:], rhs=a_f[:].rearrange("p h t -> p (h t)"), start=True, stop=True
+                    s_early[:, 256:264], lhsT=ones[:], rhs=a_f[:].rearrange("p h t -> p (h t)"), start=True, stop=True
                 )
-            if u == 10:
+            if u == SUM_AT:
                 sum_up(False)
-            if u == 11:
+            if u == SUM_AT + 1:
                 limit(False)
             if u == UNITS - 1:
                 probabilities(False)
@@ -379,23 +401,26 @@ def tile_dragonnetlogistictargetedeffect_d1p_kernel(
                 factors(False)
                 mx2(0)
             if u == UNITS + 2:
-                sum_up(True)
                 arguments(0, slice(0, C))
                 effect(0, slice(0, C), nc.gpsimd)
                 mx2(1)
-            if u == UNITS + 3:
-                limit(True)
-                probabilities(True)
             if u == UNITS + 4:
                 arguments(1, slice(0, C))
                 effect(1, slice(0, C), nc.gpsimd)
                 mx2(2)
-        factors(True)
 
         for i in range(2, TILES - 1):
+            if i == 3:
+                limit(True)
+                probabilities(True)
             mx2(i + 1)
+            asum_next(4)
             arguments(i, slice(0, C))
             effect(i, slice(0, C), nc.gpsimd)
+            if i == 2:
+                sum_up(True)
+            if i == 3:
+                factors(True)
         parts = [slice(0, C // 2), slice(C // 2, C)]
         for cols in parts:
             arguments(TILES - 1, cols)

@@ -23,18 +23,18 @@ HALF = 512
 UNITS = 16
 SPLIT = TILES // 2
 
-A_V = (5, 4, 5, 4, 0, 2, 8, 5)
-B_V = (0, 0, 0, 0, 0, 0, 1, 0)
+A_V = (4, 4, 6, 4, 3, 0, 8, 0)
+B_V = (1, 0, 0, 0, 1, 1, 1, 0)
 LEAD = 3
 WIDE = 64
 RATE = 3
-RATE_END = 5
+RATE_END = 8
 SUM_AT = 13
-QUOTA = 8
-EARLY = 3
-PERM_MID = 6
-PERM_AT = 8
-AHEAD = 20
+QUOTA = 3
+EARLY = 1
+PERM_MID = 4
+PERM_AT = 4
+AHEAD = 28
 
 
 def tile_dragonnetlogistictargetedeffect_d1p_kernel(
@@ -382,11 +382,11 @@ def tile_dragonnetlogistictargetedeffect_d1p_kernel(
                 gain(3, (u - UNITS - 1) * P, (u - UNITS) * P)
             if u + LEAD < UNITS:
                 mx1(u + LEAD)
+            asum_next(RATE if u < UNITS else RATE_END)
             if u % 2 == 0 and 2 <= u < UNITS:
                 waiting.extend((v, il) for v in (u - 2, u - 1) for il in range(4))
             if u in (UNITS - 1, UNITS):
                 waiting.extend((u - 1, il) for il in range(4))
-            asum_next(RATE if u < UNITS else RATE_END)
             if u == 3:
                 nc.tensor.matmul(
                     s_early[:, 256:264], lhsT=ones[:], rhs=a_f[:].rearrange("p h t -> p (h t)"), start=True, stop=True

from contextlib import ExitStack

import concourse.mybir as mybir
from concourse.masks import make_identity

N, D, F, C = 1024, 1024, 1024, 512
FLOPS = 2 * N * D * F + 2 * 2 * N * F * C

F32 = mybir.dt.float32
BF16 = mybir.dt.bfloat16
U32 = mybir.dt.uint32
I32 = mybir.dt.int32
U8 = mybir.dt.uint8
FP8 = mybir.dt.float8_e4m3fn
FP8X4 = mybir.dt.float8_e4m3fn_x4
FP4X4 = mybir.dt.float4_e2m1fn_x4
ALU = mybir.AluOpType
ACT = mybir.ActivationFunctionType

P = 128
TILES = N // P
HALF = 512
UNITS = 16
SPLIT = TILES // 2

A_V = (4, 4, 6, 4, 3, 0, 8, 0)
B_V = (1, 0, 0, 0, 1, 1, 1, 0)
LEAD = 3
WIDE = 64
RATE = 3
RATE_END = 8
SUM_AT = 13
QUOTA = 3
EARLY = 1
PERM_MID = 4
PERM_AT = 4
AHEAD = 28


def tile_dragonnetlogistictargetedeffect_d1p_kernel(
    tc, x_bytes, x_scale, w_words, w_scales, g, v1_words, v1_scales, v0_words, v0_scales, a, eps, out
):
    nc = tc.nc
    with ExitStack() as ctx:
        keep = ctx.enter_context(tc.tile_pool(name="keep", bufs=1))
        work = ctx.enter_context(tc.tile_pool(name="work", bufs=3))
        banks = ctx.enter_context(tc.psum_pool(name="banks", bufs=6))
        sbank = ctx.enter_context(tc.psum_pool(name="sbank", bufs=1))
        ctx.enter_context(tc.manual_schedule())

        warm = keep.tile([P, 1], F32, name="warm")
        nc.vector.memset(warm[:], 0.0)
        one = keep.tile([P, 1], F32, name="one")
        nc.vector.memset(one[:], 1.0)
        wsr = keep.tile([P, 2 * F], U8, name="wsr", align_bytes=64)
        nc.vector.memset(wsr[:].bitcast(I32), 0)
        vs = keep.tile([P, 2 * 2 * C], U8, name="vs", align_bytes=64)
        nc.vector.memset(vs[:].bitcast(I32), 0)

        x_view = x_bytes.rearrange("(p i) k -> p i k", i=TILES)
        xs = keep.tile([P, TILES, 8], F32, name="xs")
        nc.sync.dma_start(out=xs[:], in_=x_scale.rearrange("(p i) j -> p i j", i=TILES))
        xb = []
        for pr in range(4):
            xb.append(keep.tile([P, 2, D], U8, name=f"xb{pr}"))
        nc.sync.dma_start(out=xb[0][:, 0, :], in_=x_view[:, 0, :])
        nc.sync.dma_start(out=xb[0][:, 1, :], in_=x_view[:, 1, :])
        nc.sync.dma_start(out=xb[1][:], in_=x_view[:, 2:4, :])

        wr = keep.tile([P, 2, 2 * F], U8, name="wr", align_bytes=64)
        w_view = w_words.rearrange("g p b -> p g b")
        nc.scalar.dma_start(out=wr[:, :, 0:F].bitcast(I32), in_=w_view[:, :, 0:F].bitcast(I32))
        wsr_rows = wsr[:].bitcast(I32).rearrange("p (g n) -> p g n", g=2)
        ws_rows = w_scales.bitcast(I32).rearrange("g (q r) n -> r q g n", r=4)
        for r in range(4):
            nc.scalar.dma_start(out=wsr_rows[r : 128 : 32], in_=ws_rows[r])
        nc.scalar.dma_start(out=wr[:, :, F : 2 * F].bitcast(I32), in_=w_view[:, :, F : 2 * F].bitcast(I32))
        nc.scalar.activation(out=warm[:], in_=warm[:], func=ACT.Exp)

        a_bf = keep.tile([P, 2, 4], BF16, name="a_bf")
        g_bf = keep.tile([P, 2, 4], BF16, name="g_bf")
        nc.sync.dma_start(out=a_bf[:], in_=a.rearrange("(h p t) -> p h t", p=P, t=4))
        nc.sync.dma_start(out=g_bf[:], in_=g.rearrange("(h p t) -> p h t", p=P, t=4))
        nc.sync.dma_start(out=xb[2][:], in_=x_view[:, 4:6, :])
        nc.sync.dma_start(out=xb[3][:], in_=x_view[:, 6:8, :])
        vw = keep.tile([P, 2, 2, 2 * C], U8, name="vw", align_bytes=64)
        nc.sync.dma_start(out=vw[:, :, 0, :], in_=v1_words.rearrange("g p b -> p g b"))
        nc.sync.dma_start(out=vw[:, :, 1, :], in_=v0_words.rearrange("g p b -> p g b"))
        vs_rows = vs[:].bitcast(I32).rearrange("p (v g n) -> p v g n", v=2, g=2)
        for v, src in ((0, v1_scales), (1, v0_scales)):
            src_rows = src.bitcast(I32).rearrange("g (q r) n -> r q g n", r=4)
            for r in range(4):
                nc.sync.dma_start(out=vs_rows[r : 128 : 32, v], in_=src_rows[r])
        eps_b = keep.tile([P, C], BF16, name="eps_b")
        nc.sync.dma_start(out=eps_b[:], in_=eps.partition_broadcast(P))

        ident = keep.tile([P, P], F32, name="ident")
        make_identity(nc, ident[:])
        a_f = keep.tile([P, 2, 4], F32, name="a_f")
        ones = keep.tile([P, P], F32, name="ones")
        nc.gpsimd.memset(ones[:], 1.0)

        wp = keep.tile([P, 2, 2, 4, 256], U8, name="wp", align_bytes=64)
        wsp = keep.tile([P, 2, 2, 4, 128], U8, name="wsp", align_bytes=64)
        xin = [keep.tile([P, 2, HALF * 4], BF16, name=f"xin{h}", align_bytes=64) for h in range(2)]
        xq = [keep.tile([P, 2, HALF], U32, name=f"xq{h}", align_bytes=64) for h in range(2)]
        xqs = [keep.tile([P, 2, HALF], U8, name=f"xqs{h}", align_bytes=64) for h in range(2)]
        zq = [keep.tile([P, 2, HALF], U32, name=f"zq{h}", align_bytes=64) for h in range(2)]
        zqs = [keep.tile([P, 2, HALF], U8, name=f"zqs{h}", align_bytes=64) for h in range(2)]
        s_early = sbank.tile([P, 512], F32, name="s_early")
        s_late = sbank.tile([P, 512], F32, name="s_late")

        xw = {}
        t_of = {}
        bank_of = {}
        e_of = {}
        y1_of = {}
        h_of = {}
        zin_of = {}

        def widen(i, j, on_vector):
            if i not in xw:
                xw[i] = work.tile([P, D], BF16, name="xw", bufs=4, align_bytes=64)
            src = xb[i // 2][:, i % 2, j * P : (j + 1) * P].bitcast(FP8)
            dst = xw[i][:, j * P : (j + 1) * P]
            if on_vector:
                nc.vector.tensor_scalar(out=dst, in0=src, scalar1=xs[:, i, j : j + 1], scalar2=None, op0=ALU.mult)
            else:
                nc.scalar.activation(out=dst, in_=src, func=ACT.Copy, scale=xs[:, i, j : j + 1])

        def turn(i):
            bank = banks.tile([P, 512], F32, name="bank")
            t_of[i] = bank
            words = xw[i][:].bitcast(F32)
            for gg in range(2):
                for u in range(2):
                    c = (2 * gg + u) * P
                    nc.tensor.transpose(bank[:, c : c + P], words[:, 256 * gg + u : 256 * (gg + 1) : 2], ident[:])

        def untangle(i, on_vector):
            half, il = divmod(i, 4)
            dst = xin[half][:].bitcast(F32).rearrange("p g (n u) -> p g n u", u=2)[:, :, il * P : (il + 1) * P, :]
            src = t_of[i][:].rearrange("p (g u n) -> p g n u", g=2, u=2)
            if on_vector:
                nc.vector.tensor_copy(out=dst, in_=src)
            else:
                nc.scalar.copy(out=dst, in_=src)

        def quant_x(pair):
            half, pl = divmod(pair, 2)
            for gg in range(2):
                nc.vector.quantize_mx(
                    out=xq[half][:, gg, pl * 256 : (pl + 1) * 256].bitcast(FP8X4),
                    scales=xqs[half][:, gg, pl * 256 : (pl + 1) * 256],
                    in_=xin[half][:, gg, pl * 1024 : (pl + 1) * 1024],
                )

        def permute_w(k, engine):
            G, t = divmod(k, 4)
            src = wr[:, :, G * F : (G + 1) * F].rearrange("p g (m t b) -> p g t m b", t=4, b=2)[:, :, t]
            engine.tensor_copy(out=wp[:, :, G, t, :].rearrange("p g (m b) -> p g m b", b=2), in_=src)
            src = wsr[:].rearrange("p (g h m t) -> p g h t m", g=2, h=2, t=4)[:, :, G, t]
            engine.tensor_copy(out=wsp[:, :, G, t, :], in_=src)

        def mx1(u):
            half, k = divmod(u, 8)
            G, t = divmod(k, 4)
            bank = banks.tile([P, 512], F32, name="bank")
            bank_of[u] = bank
            for gg in range(2):
                nc.tensor.matmul_mx(
                    out=bank[:],
                    lhsT=wp[:, gg, G, t, :].bitcast(FP4X4),
                    lhsT_scale=wsp[:, gg, G, t, :],
                    rhs=xq[half][:, gg, :].bitcast(FP8X4),
                    rhs_scale=xqs[half][:, gg, :],
                    start=gg == 0,
                    stop=gg == 1,
                )

        def exp(u):
            pair, k = divmod(u, 2)
            if k == 0:
                e_of[pair] = work.tile([P, 2, HALF], F32, name="e")
                y1_of[pair] = work.tile([P, 2, HALF], F32, name="y1")
            nc.scalar.activation(out=e_of[pair][:, k, :], in_=bank_of[u][:], func=ACT.Exp)
            nc.scalar.activation(out=y1_of[pair][:, k, :], in_=bank_of[u][:], func=ACT.Identity, bias=one[:])

        def elu1(pair, part):
            grp, k = divmod(pair, 2)
            if k == 0 and part.start == 0:
                h_of[grp] = work.tile([P, 4, HALF], F32, name="h", bufs=4)
            nc.vector.scalar_tensor_tensor(
                out=h_of[grp][:, 2 * k + part.start : 2 * k + part.stop, :],
                in0=e_of[pair][:, part, :],
                scalar=1.0,
                in1=y1_of[pair][:, part, :],
                op0=ALU.min,
                op1=ALU.max,
            )

        def asum(u, il):
            grp, t = divmod(u, 4)
            half, G = divmod(grp, 2)
            sums = (s_early, s_late)[half]
            if True:
                col = (4 * G + t) * 4 + il
                nc.tensor.matmul(
                    sums[:, col : col + WIDE],
                    lhsT=h_of[grp][:, t, il * P : (il + 1) * P],
                    rhs=a_f[:, G, t : t + 1].to_broadcast([P, WIDE]),
                    start=True,
                    stop=True,
                )

        def gain(grp, lo, hi):
            G = grp % 2
            if lo == 0:
                zin_of[grp] = work.tile([P, HALF, 4], BF16, name="zin", align_bytes=64)
            nc.vector.scalar_tensor_tensor(
                out=zin_of[grp][:, lo:hi, :],
                in0=h_of[grp][:].rearrange("p t n -> p n t")[:, lo:hi, :],
                scalar=-1.0,
                in1=g_bf[:, G : G + 1, :].to_broadcast([P, hi - lo, 4]),
                op0=ALU.add,
                op1=ALU.mult,
            )

        def quant_z(grp, lo, hi):
            half, G = divmod(grp, 2)
            nc.vector.quantize_mx(
                out=zq[half][:, G, lo:hi].bitcast(FP8X4),
                scales=zqs[half][:, G, lo:hi],
                in_=zin_of[grp][:, lo:hi, :].rearrange("p n t -> p (n t)"),
            )

        blocks = [(i, j) for i in range(TILES) for j in range(8)]
        turned = []
        copied = []

        def widen_next(quota):
            while blocks and quota > 0:
                i, j = blocks.pop(0)
                widen(i, j, j < A_V[i])
                quota -= 1
                if j == 7:
                    turn(i)
                    turned.append(i)

        for k in range(PERM_AT, 8):
            permute_w(k, nc.gpsimd)
        widen_next(32)
        for k in range(EARLY):
            permute_w(k, nc.vector)
        for i in range(4):
            untangle(i, B_V[i] == 1)
            if i == 2:
                quant_x(0)
        turned.clear()
        quant_x(1)
        for k in range(EARLY, PERM_MID):
            permute_w(k, nc.vector)
        nc.vector.tensor_copy(out=a_f[:], in_=a_bf[:])
        for u in range(LEAD):
            mx1(u)
        for k in range(PERM_MID, PERM_AT):
            permute_w(k, nc.vector)
        widen_next(AHEAD)

        rr = keep.tile([P, 2, 2, 4], F32, name="rr")
        nr = keep.tile([P, 2, 4], F32, name="nr")
        sum_of = {}
        lim_of = {}
        prob_of = {}

        def sum_up(late):
            assert not [w for w in waiting if w[0] // 8 == late]
            sums = s_late if late else s_early
            sum_of[late] = keep.tile([P, 5], F32, name="sum_late" if late else "sum_early")
            nc.vector.tensor_reduce(
                out=sum_of[late][:, 0:4],
                in_=sums[:, 0:32].rearrange("p (k i) -> p i k", i=4),
                axis=mybir.AxisListType.X,
                op=ALU.add,
            )
            if not late:
                nc.vector.tensor_reduce(
                    out=sum_of[late][:, 4:5], in_=sums[:, 256:264], axis=mybir.AxisListType.X, op=ALU.add
                )

        def limit(late):
            total = sum_of[False][:, 4:5]
            lim = keep.tile([P, 2, 4], F32, name="lim_late" if late else "lim_early")
            lim_of[late] = lim
            for v, (bound, op) in enumerate(((-86.0, ALU.max), (86.0, ALU.min))):
                nc.vector.tensor_scalar(
                    out=lim[:, v, :], in0=sum_of[late][:, 0:4], scalar1=total, scalar2=bound, op0=ALU.subtract, op1=op
                )

        def probabilities(late):
            prob = keep.tile([P, 2, 4], F32, name="prob_late" if late else "prob_early")
            prob_of[late] = prob
            for v, sign in enumerate((1.0, -1.0)):
                nc.scalar.activation(out=prob[:, v, :], in_=lim_of[late][:, v, :], func=ACT.Sigmoid, scale=sign)

        def factors(late):
            rec = rr[:, late, :, :]
            nc.vector.reciprocal(out=rec, in_=prob_of[late][:])
            nc.vector.tensor_scalar(out=nr[:, late, :], in0=rr[:, late, 1, :], scalar1=-1.0, scalar2=None, op0=ALU.mult)

        out_view = out.rearrange("(p i) c -> p i c", i=TILES)
        vs_view = vs[:].rearrange("p (v g n) -> p v g n", v=2, g=2)
        q_of = {}
        arg_of = {}

        def mx2(i):
            for v in range(2):
                bank = banks.tile([P, 512], F32, name="bank")
                q_of[i, v] = bank
                for G in range(2):
                    nc.tensor.matmul_mx(
                        out=bank[:],
                        lhsT=zq[i // 4][:, G, i % 4 * P : (i % 4 + 1) * P].bitcast(FP8X4),
                        lhsT_scale=zqs[i // 4][:, G, i % 4 * P : (i % 4 + 1) * P],
                        rhs=vw[:, G, v, :].bitcast(FP4X4),
                        rhs_scale=vs_view[:, v, G, :],
                        start=G == 0,
                        stop=G == 1,
                    )

        def arguments(i, cols):
            late, il = divmod(i, 4)
            arg = work.tile([P, 2, cols.stop - cols.start], F32, name="arg", bufs=4)
            arg_of[i, cols.start] = arg
            for v, factor in enumerate((rr[:, late, 0, il : il + 1], nr[:, late, il : il + 1])):
                nc.vector.scalar_tensor_tensor(
                    out=arg[:, v, :], in0=eps_b[:, cols], scalar=factor, in1=q_of[i, v][:, cols],
                    op0=ALU.mult, op1=ALU.add,
                )

        def effect(i, cols, engine):
            width = cols.stop - cols.start
            tt = work.tile([P, 2, width], F32, name="tt", bufs=4)
            nc.scalar.activation(out=tt[:], in_=arg_of[i, cols.start][:], func=ACT.Sigmoid)
            o = work.tile([P, width], F32, name="o", bufs=9)
            engine.tensor_sub(out=o[:], in0=tt[:, 0, :], in1=tt[:, 1, :])
            nc.sync.dma_start(out=out_view[:, i, cols], in_=o[:])

        waiting = []

        def asum_next(quota):
            while waiting and quota > 0:
                u, il = waiting.pop(0)
                asum(u, il)
                quota -= 1

        for u in range(UNITS + 6):
            if u < UNITS:
                exp(u)
            for i in turned:
                untangle(i, B_V[i] == 1)
                copied.append(i)
            turned.clear()
            widen_next(QUOTA)
            last = u > UNITS
            if u % 2 == 0 and 2 <= u < UNITS:
                elu1(u // 2 - 1, slice(0, 2))
            if u in (UNITS - 1, UNITS):
                elu1(UNITS // 2 - 1, slice(u - UNITS + 1, u - UNITS + 2))
            piece, odd = divmod(u - 5, 2)
            if odd == 1 and 0 <= piece < 6:
                quant_z(piece // 2, (piece % 2) * 256, (piece % 2 + 1) * 256)
            if UNITS + 2 <= u < UNITS + 6:
                quant_z(3, (u - UNITS - 2) * P, (u - UNITS - 1) * P)
            for i in copied:
                if i % 2 == 1:
                    quant_x(i // 2)
            copied.clear()
            if odd == 0 and 0 <= piece < 6:
                gain(piece // 2, (piece % 2) * 256, (piece % 2 + 1) * 256)
            if UNITS + 1 <= u < UNITS + 5:
                gain(3, (u - UNITS - 1) * P, (u - UNITS) * P)
            if u + LEAD < UNITS:
                mx1(u + LEAD)
            asum_next(RATE if u < UNITS else RATE_END)
            if u % 2 == 0 and 2 <= u < UNITS:
                waiting.extend((v, il) for v in (u - 2, u - 1) for il in range(4))
            if u in (UNITS - 1, UNITS):
                waiting.extend((u - 1, il) for il in range(4))
            if u == 3:
                nc.tensor.matmul(
                    s_early[:, 256:264], lhsT=ones[:], rhs=a_f[:].rearrange("p h t -> p (h t)"), start=True, stop=True
                )
            if u == SUM_AT:
                sum_up(False)
            if u == SUM_AT + 1:
                limit(False)
            if u == UNITS - 1:
                probabilities(False)
            if u == UNITS + 1:
                factors(False)
                mx2(0)
            if u == UNITS + 2:
                arguments(0, slice(0, C))
                effect(0, slice(0, C), nc.gpsimd)
                mx2(1)
            if u == UNITS + 4:
                arguments(1, slice(0, C))
                effect(1, slice(0, C), nc.gpsimd)
                mx2(2)

        for i in range(2, TILES - 1):
            if i == 3:
                limit(True)
                probabilities(True)
            mx2(i + 1)
            asum_next(4)
            arguments(i, slice(0, C))
            effect(i, slice(0, C), nc.gpsimd)
            if i == 2:
                sum_up(True)
            if i == 3:
                factors(True)
        parts = [slice(0, C // 2), slice(C // 2, C)]
        for cols in parts:
            arguments(TILES - 1, cols)
        for cols in parts:
            effect(TILES - 1, cols, nc.vector)
